import numpy as np
import ml_dtypes


def mxq(x, axis, fmt="e4m3"):
    dtype, down = {"e4m3": (ml_dtypes.float8_e4m3fn, 7), "e5m2": (ml_dtypes.float8_e5m2, 14)}[fmt]
    v = np.moveaxis(np.asarray(x, np.float32).astype(ml_dtypes.bfloat16).astype(np.float64), axis, -1)
    blocks = v.reshape(v.shape[:-1] + (-1, 32))
    amax = np.abs(blocks).max(-1, keepdims=True)
    byte = np.maximum(np.where(amax > 0, np.frexp(amax)[1] - 1 + 127, 0) - down, 1)
    scale = np.exp2(byte - 127.0)
    codes = (blocks / scale).astype(np.float32).astype(dtype).astype(np.float64)
    return np.moveaxis((codes * scale).reshape(v.shape), -1, axis)


WIDE = False


def mx_kscale(k):
    if not WIDE:
        return np.ones(k)
    levels = np.array([30, -30])
    if k % 512:
        return np.exp2(np.random.permutation(np.resize(levels, k // 32))).repeat(32)
    a = np.empty((k // 512, 16))
    for p in range(k // 512):
        a[p, :8] = np.random.permutation(np.resize(levels, 8))
        for g in range(8):
            far = levels[np.abs(levels - a[p, g]) >= 10]
            a[p, g + 8] = far[np.random.randint(len(far))]
    return np.exp2(a.ravel()).repeat(32)


def f64(x):
    return np.asarray(x).astype(np.float64)


E2M1 = np.array([0.0, 0.5, 1.0, 1.5, 2.0, 3.0, 4.0, 6.0, -0.0, -0.5, -1.0, -1.5, -2.0, -3.0, -4.0, -6.0])


def pack_weight(w, fmt):
    k, n = w.shape
    w = f64(np.asarray(w, np.float32).astype(ml_dtypes.bfloat16)).reshape(k // 32, 32, n)
    amax = np.abs(w).max(1)
    if fmt == "e4m3":
        byte = np.frexp(amax)[1] - 1 + 127 - 7
    else:
        mant, ex = np.frexp(amax / 6.0)
        byte = np.where(mant > 0.5, ex, ex - 1) + 127
    byte = np.clip(np.where(amax > 0, byte, 1), 1, 254)
    scaled = (w * np.exp2(127.0 - byte)[:, None, :]).reshape(k, n).astype(np.float32)
    by_word = np.ascontiguousarray(scaled.reshape(k // 512, 128, 4, n).transpose(0, 1, 3, 2))
    if fmt == "e4m3":
        words = by_word.astype(ml_dtypes.float8_e4m3fn).view(np.uint8)
    else:
        c = by_word.astype(ml_dtypes.float4_e2m1fn).view(np.uint8) & 0xF
        words = (c[..., 0::2] | (c[..., 1::2] << 4)).reshape(k // 512, 128, 2 * n)
    return np.ascontiguousarray(words), np.ascontiguousarray(byte.astype(np.uint8).reshape(k // 512, 16, n))


def unpack_weight(words, scales, fmt):
    g, _, n = scales.shape
    words = np.ascontiguousarray(words).reshape(g, 128, n, -1)
    if fmt == "e4m3":
        vals = words.view(ml_dtypes.float8_e4m3fn).astype(np.float64)
    else:
        nib = np.empty((g, 128, n, 4), np.uint8)
        nib[..., 0::2] = words & 0xF
        nib[..., 1::2] = words >> 4
        vals = E2M1[nib]
    vals = vals * np.repeat(np.exp2(scales.astype(np.float64) - 127.0), 8, axis=1)[..., None]
    return vals.transpose(0, 1, 3, 2).reshape(g * 512, n)


def bf(x):
    return np.asarray(x, np.float32).astype(ml_dtypes.bfloat16)


def planes(Y):
    r, m = Y.shape
    b = f64(bf(Y)).reshape(r // 32, 32, m)
    amax = np.abs(b).max(1)
    byte = np.clip(np.where(amax > 0, np.frexp(amax)[1] - 1 + 127 - 7, 1), 1, 254)
    codes = (b * np.exp2(127.0 - byte)[:, None, :]).reshape(r, m).astype(np.float32).astype(ml_dtypes.float8_e4m3fn).view(np.uint8)
    words = codes.reshape(r // 512, 128, 4, m).transpose(0, 1, 3, 2)
    return np.ascontiguousarray(words), np.ascontiguousarray(byte.astype(np.uint8).reshape(r // 512, 16, m))


K, R, T, S, N = 1024, 512, 512, 512, 512


def setup_inputs():
    n = np.random.standard_normal
    fk = mx_kscale(K)
    ft = mx_kscale(T)
    fs = mx_kscale(S)
    xtp = pack_weight(n((K, T)) / fk[:, None], "e2m1")
    wap = pack_weight(n((K, R)) * 1 / np.sqrt(K) * fk[:, None], "e4m3")
    hsp = pack_weight(n((S, R)) * fs[:, None], "e2m1")
    gsp = pack_weight(n((S, N)) / fs[:, None], "e4m3")
    return {
        "xt_words": xtp[0],
        "xt_scales": xtp[1],
        "wa_words": wap[0],
        "wa_scales": wap[1],
        "rw": (np.random.uniform(0.5, 1.5, (1, T)) * ft).astype(np.float32),
        "g": (n((T, N)) * np.exp(0.5 * n((T, 1))) / ft[:, None]).astype(np.float32),
        "hs_words": hsp[0],
        "hs_scales": hsp[1],
        "gs_words": gsp[0],
        "gs_scales": gsp[1],
    }


def reference(xt_words, xt_scales, wa_words, wa_scales, rw, g, hs_words, hs_scales, gs_words, gs_scales):
    xtu = unpack_weight(xt_words, xt_scales, "e2m1")
    wau = unpack_weight(wa_words, wa_scales, "e4m3")
    hsu = unpack_weight(hs_words, hs_scales, "e2m1")
    gsu = unpack_weight(gs_words, gs_scales, "e4m3")
    a = wau.T @ xtu
    h1 = np.maximum(a, 0.0) * f64(rw)
    ht = h1.T
    htq = mxq(ht, 0, "e4m3")
    gq = mxq(f64(g), 0, "e5m2")
    w = htq.T @ gq + hsu.T @ gsu
    y = 0.04 * w
    words, scales = planes(y)
    return y, words, scales

@@ -1,0 +1,219 @@
+from contextlib import ExitStack
+
+import concourse.mybir as mybir
+
+K, R, T, S, N = 1024, 512, 512, 512, 512
+FLOPS = 2 * (K * R * T + T * R * N + S * R * N)
+
+F32 = mybir.dt.float32
+BF16 = mybir.dt.bfloat16
+I32 = mybir.dt.int32
+U32 = mybir.dt.uint32
+U8 = mybir.dt.uint8
+E4M3 = mybir.dt.float8_e4m3fn_x4
+E5M2 = mybir.dt.float8_e5m2_x4
+E2M1 = mybir.dt.float4_e2m1fn_x4
+ALU = mybir.AluOpType
+ACT = mybir.ActivationFunctionType
+
+P = 128
+PACK = 4
+PASSES = K // (P * PACK)
+QUADS = 4
+OUT_FACTOR = 0.04
+HALF = N // 2
+VECTOR_COLS = 344
+
+
+def tile_mix_wgrad_of_hidden_and_store_pl_kernel(
+    tc, xt_words, xt_scales, wa_words, wa_scales, rw, g, hs_words, hs_scales, gs_words, gs_scales, out_0, out_1, out_2
+):
+    nc = tc.nc
+    with ExitStack() as ctx:
+        sb = ctx.enter_context(tc.tile_pool(name="sb", bufs=1))
+        psum = ctx.enter_context(tc.psum_pool(name="psum", bufs=1))
+        ctx.enter_context(tc.manual_schedule())
+
+        def tile(name, shape, dtype):
+            return sb.tile(shape, dtype, name=name, align_bytes=64)
+
+        xt_raw = tile("xt_raw", [P, PASSES, 2 * T], U8)
+        xt_dealt = tile("xt_dealt", [P, PACK, PASSES, 2 * P], U8)
+        xs_raw = tile("xs_raw", [P, PASSES, T], U8)
+        xs_dealt = tile("xs_dealt", [P, PACK, PASSES, P], U8)
+        wa_codes = tile("wa_codes", [P, PASSES, R], U32)
+        wa_plane = tile("wa_plane", [P, PASSES, R], U8)
+        rw_sb = tile("rw_sb", [P, PACK], F32)
+        g_raw = [tile("g_raw%d" % h, [P, PACK, HALF], F32) for h in range(2)]
+        g_bf = tile("g_bf", [P, N, PACK], BF16)
+        g_codes = tile("g_codes", [P, N], U32)
+        g_plane = tile("g_plane", [P, N], U8)
+        hs_raw = tile("hs_raw", [P, 2 * R], U8)
+        hs_dealt = tile("hs_dealt", [P, PACK, 2 * P], U8)
+        hss_raw = tile("hss_raw", [P, 1, R], U8)
+        hss_dealt = tile("hss_dealt", [P, PACK, P], U8)
+        gs_codes = tile("gs_codes", [P, N], U32)
+        gs_plane = tile("gs_plane", [P, 1, N], U8)
+        ht_bf = tile("ht_bf", [P, PACK, P, PACK], BF16)
+        ht_codes = tile("ht_codes", [P, PACK, P], U32)
+        ht_plane = tile("ht_plane", [P, PACK, P], U8)
+        y = tile("y", [P, PACK, N], F32)
+        y_bf = tile("y_bf", [P, N, PACK], BF16)
+        y_codes = tile("y_codes", [P, N], U32)
+        y_plane = tile("y_plane", [P, N], U8)
+        a_ps = [psum.tile([P, PACK, P], F32, name="a_ps%d" % b) for b in range(PACK)]
+        w_ps = [psum.tile([P, N], F32, name="w_ps%d" % i) for i in range(PACK)]
+
+        def load_scale_rows(queue, plane, scales, q):
+            queue.dma_start(
+                out=plane[32 * q : 32 * q + 4].bitcast(I32),
+                in_=scales[:, 4 * q : 4 * q + 4, :].rearrange("z r c -> r z c").bitcast(I32),
+            )
+
+        def load_g(h):
+            nc.sync.dma_start(
+                out=g_raw[h][:], in_=g.rearrange("(p j) n -> p j n", j=PACK)[:, :, h * HALF : (h + 1) * HALF]
+            )
+
+        for plane in (xs_raw, wa_plane, hss_raw, gs_plane):
+            nc.vector.memset(plane[:].bitcast(U32), 0)
+
+        nc.sync.dma_start(out=xt_raw[:].bitcast(I32), in_=xt_words.rearrange("z p c -> p z c").bitcast(I32))
+        nc.sync.dma_start(out=rw_sb[:], in_=rw.rearrange("o (p j) -> p (o j)", j=PACK))
+        load_scale_rows(nc.sync, xs_raw, xt_scales, 0)
+        load_scale_rows(nc.scalar, xs_raw, xt_scales, 2)
+        load_scale_rows(nc.sync, xs_raw, xt_scales, 1)
+        load_scale_rows(nc.scalar, xs_raw, xt_scales, 3)
+        nc.sync.dma_start(out=wa_codes[:].bitcast(I32), in_=wa_words.rearrange("z p c t -> p z (c t)").bitcast(I32))
+        for q in range(QUADS):
+            load_scale_rows(nc.scalar, wa_plane, wa_scales, q)
+        nc.sync.dma_start(out=hs_raw[:].bitcast(I32), in_=hs_words[0].bitcast(I32))
+        load_g(0)
+        for q in range(QUADS):
+            load_scale_rows(nc.scalar, hss_raw, hs_scales, q)
+        load_g(1)
+        nc.sync.dma_start(out=gs_codes[:].bitcast(I32), in_=gs_words[0].rearrange("p c t -> p (c t)").bitcast(I32))
+        for q in range(QUADS):
+            load_scale_rows(nc.sync, gs_plane, gs_scales, q)
+
+        nc.vector.tensor_copy(
+            out=xs_dealt[:].rearrange("p j z (h l) -> p (z h) j l", l=16),
+            in_=xs_raw[:].rearrange("p z (h l j) -> p (z h) j l", l=16, j=PACK),
+        )
+        nc.vector.tensor_copy(
+            out=xt_dealt[:].rearrange("p j z (h l b) -> p (z h) j l b", l=8, b=2),
+            in_=xt_raw[:].rearrange("p z (h l j b) -> p (z h) j l b", l=8, j=PACK, b=2),
+        )
+        nc.vector.tensor_copy(
+            out=hs_dealt[:].rearrange("p i (h l b) -> p h i l b", l=8, b=2),
+            in_=hs_raw[:].rearrange("p (h l i b) -> p h i l b", l=8, i=PACK, b=2),
+        )
+
+        def interleave(copy, dst, src):
+            copy(
+                out=dst.rearrange("p (c e) t -> p c t e", e=4),
+                in_=src.rearrange("p t (c e) -> p c t e", e=4),
+            )
+
+        def scalar_cast(out, in_):
+            nc.scalar.activation(out=out, in_=in_, func=ACT.Copy)
+
+        def quantize(codes, plane, src, fmt):
+            nc.vector.quantize_mx(out=codes.bitcast(fmt), scales=plane, in_=src.rearrange("p c t -> p (c t)"))
+
+        def first_layer(b):
+            cols = slice(b * P, (b + 1) * P)
+            for j in range(PACK):
+                for z in range(PASSES):
+                    nc.tensor.matmul_mx(
+                        out=a_ps[b][:, j, :],
+                        lhsT=xt_dealt[:, j, z, :].bitcast(E2M1),
+                        lhsT_scale=xs_dealt[:, j, z, :],
+                        rhs=wa_codes[:, z, cols].bitcast(E4M3),
+                        rhs_scale=wa_plane[:, z, cols],
+                        start=(z == 0),
+                        stop=(z == PASSES - 1),
+                    )
+
+        per_bank = P // PACK
+
+        def hidden(b, i):
+            nc.vector.scalar_tensor_tensor(
+                out=ht_bf[:, i, b * per_bank : (b + 1) * per_bank, :],
+                in0=a_ps[b][:].rearrange("p j (m i) -> p i m j", i=PACK)[:, i],
+                scalar=0.0,
+                in1=rw_sb[:].unsqueeze(1).to_broadcast([P, per_bank, PACK]),
+                op0=ALU.max,
+                op1=ALU.mult,
+            )
+
+        def quantize_g(h):
+            cols = slice(h * HALF, (h + 1) * HALF)
+            quantize(g_codes[:, cols], g_plane[:, cols], g_bf[:, cols, :], E5M2)
+
+        def quantize_ht(i):
+            quantize(ht_codes[:, i, :], ht_plane[:, i, :], ht_bf[:, i], E4M3)
+
+        for h in range(2):
+            interleave(scalar_cast, g_bf[:, h * HALF : (h + 1) * HALF, :], g_raw[h][:])
+
+        for b in range(PACK - 1):
+            first_layer(b)
+            for i in range(PACK):
+                hidden(b, i)
+            if b == 0:
+                nc.vector.tensor_copy(
+                    out=hss_dealt[:].rearrange("p i (h l) -> p h i l", l=16),
+                    in_=hss_raw[:, 0, :].rearrange("p (h l i) -> p h i l", l=16, i=PACK),
+                )
+        quantize_g(0)
+        first_layer(PACK - 1)
+        for i in range(PACK):
+            nc.tensor.matmul_mx(
+                out=w_ps[i][:],
+                lhsT=hs_dealt[:, i, :].bitcast(E2M1),
+                lhsT_scale=hss_dealt[:, i, :],
+                rhs=gs_codes[:].bitcast(E4M3),
+                rhs_scale=gs_plane[:, 0, :],
+                start=True,
+                stop=False,
+            )
+        for i in range(PACK):
+            hidden(PACK - 1, i)
+            if i > 0:
+                quantize_ht(i - 1)
+        quantize_g(1)
+        quantize_ht(PACK - 1)
+
+        out_rows = out_0.rearrange("(p i) n -> p i n", i=PACK)
+        for i in range(PACK):
+            nc.tensor.matmul_mx(
+                out=w_ps[i][:],
+                lhsT=ht_codes[:, i, :].bitcast(E4M3),
+                lhsT_scale=ht_plane[:, i, :],
+                rhs=g_codes[:].bitcast(E5M2),
+                rhs_scale=g_plane[:],
+                start=False,
+                stop=True,
+            )
+            if i % 2 == 0:
+                nc.scalar.activation(out=y[:, i, :], in_=w_ps[i][:], func=ACT.Copy, scale=OUT_FACTOR)
+            else:
+                nc.vector.tensor_scalar(
+                    out=y[:, i, :], in0=w_ps[i][:], scalar1=OUT_FACTOR, scalar2=None, op0=ALU.mult
+                )
+            nc.sync.dma_start(out=out_rows[:, i, :], in_=y[:, i, :])
+
+        interleave(scalar_cast, y_bf[:, VECTOR_COLS:, :], y[:, :, VECTOR_COLS:])
+        interleave(nc.vector.tensor_copy, y_bf[:, :HALF, :], y[:, :, :HALF])
+        interleave(nc.vector.tensor_copy, y_bf[:, HALF:VECTOR_COLS, :], y[:, :, HALF:VECTOR_COLS])
+        word_rows = out_1[0].rearrange("p c t -> p (c t)").bitcast(I32)
+        for h in range(2):
+            cols = slice(h * HALF, (h + 1) * HALF)
+            quantize(y_codes[:, cols], y_plane[:, cols], y_bf[:, cols, :], E4M3)
+            nc.sync.dma_start(out=word_rows[:, cols], in_=y_codes[:, cols].bitcast(I32))
+        for q in range(QUADS):
+            queue = nc.scalar if q % 2 == 0 else nc.sync
+            queue.dma_start(
+                out=out_2[0, 4 * q : 4 * q + 4, :].bitcast(I32), in_=y_plane[32 * q : 32 * q + 4, :].bitcast(I32)
+            )

@@ -22,7 +22,8 @@ PASSES = K // (P * PACK)
 QUADS = 4
 OUT_FACTOR = 0.04
 HALF = N // 2
-VECTOR_COLS = 344
+VECTOR_COLS = 384
+WARM_PASSES = 4
 
 
 def tile_mix_wgrad_of_hidden_and_store_pl_kernel(
@@ -61,6 +62,9 @@ def tile_mix_wgrad_of_hidden_and_store_pl_kernel(
         y_bf = tile("y_bf", [P, N, PACK], BF16)
         y_codes = tile("y_codes", [P, N], U32)
         y_plane = tile("y_plane", [P, N], U8)
+        warm_bf = tile("warm_bf", [P, P, PACK], BF16)
+        warm_codes = tile("warm_codes", [P, N + P], U32)
+        warm_plane = tile("warm_plane", [P, N + P], U8)
         a_ps = [psum.tile([P, PACK, P], F32, name="a_ps%d" % b) for b in range(PACK)]
         w_ps = [psum.tile([P, N], F32, name="w_ps%d" % i) for i in range(PACK)]
 
@@ -75,34 +79,58 @@ def tile_mix_wgrad_of_hidden_and_store_pl_kernel(
                 out=g_raw[h][:], in_=g.rearrange("(p j) n -> p j n", j=PACK)[:, :, h * HALF : (h + 1) * HALF]
             )
 
-        for plane in (xs_raw, wa_plane, hss_raw, gs_plane):
+        for plane in (xs_raw, wa_plane):
+            nc.vector.memset(plane[:].bitcast(U32), 0)
+        nc.vector.memset(warm_bf[:].rearrange("p c t -> p (c t)").bitcast(U32), 0)
+        for plane in (hss_raw, gs_plane):
             nc.vector.memset(plane[:].bitcast(U32), 0)
 
         nc.sync.dma_start(out=xt_raw[:].bitcast(I32), in_=xt_words.rearrange("z p c -> p z c").bitcast(I32))
-        nc.sync.dma_start(out=rw_sb[:], in_=rw.rearrange("o (p j) -> p (o j)", j=PACK))
-        load_scale_rows(nc.sync, xs_raw, xt_scales, 0)
-        load_scale_rows(nc.scalar, xs_raw, xt_scales, 2)
-        load_scale_rows(nc.sync, xs_raw, xt_scales, 1)
-        load_scale_rows(nc.scalar, xs_raw, xt_scales, 3)
-        nc.sync.dma_start(out=wa_codes[:].bitcast(I32), in_=wa_words.rearrange("z p c t -> p z (c t)").bitcast(I32))
         for q in range(QUADS):
-            load_scale_rows(nc.scalar, wa_plane, wa_scales, q)
+            load_scale_rows(nc.scalar if q % 2 == 0 else nc.sync, xs_raw, xt_scales, q)
+        load_scale_rows(nc.scalar, wa_plane, wa_scales, 0)
+        load_scale_rows(nc.sync, wa_plane, wa_scales, 1)
+        nc.sync.dma_start(out=wa_codes[:].bitcast(I32), in_=wa_words.rearrange("z p c t -> p z (c t)").bitcast(I32))
+        load_scale_rows(nc.sync, wa_plane, wa_scales, 2)
+        load_scale_rows(nc.sync, wa_plane, wa_scales, 3)
+        nc.sync.dma_start(out=rw_sb[:], in_=rw.rearrange("o (p j) -> p (o j)", j=PACK))
         nc.sync.dma_start(out=hs_raw[:].bitcast(I32), in_=hs_words[0].bitcast(I32))
         load_g(0)
-        for q in range(QUADS):
-            load_scale_rows(nc.scalar, hss_raw, hs_scales, q)
+        load_scale_rows(nc.sync, hss_raw, hs_scales, 0)
+        load_scale_rows(nc.sync, hss_raw, hs_scales, 1)
         load_g(1)
+        load_scale_rows(nc.sync, hss_raw, hs_scales, 2)
+        load_scale_rows(nc.sync, hss_raw, hs_scales, 3)
+        load_scale_rows(nc.sync, gs_plane, gs_scales, 0)
+        load_scale_rows(nc.sync, gs_plane, gs_scales, 1)
         nc.sync.dma_start(out=gs_codes[:].bitcast(I32), in_=gs_words[0].rearrange("p c t -> p (c t)").bitcast(I32))
-        for q in range(QUADS):
-            load_scale_rows(nc.sync, gs_plane, gs_scales, q)
+        load_scale_rows(nc.sync, gs_plane, gs_scales, 2)
+        load_scale_rows(nc.sync, gs_plane, gs_scales, 3)
 
-        nc.vector.tensor_copy(
-            out=xs_dealt[:].rearrange("p j z (h l) -> p (z h) j l", l=16),
-            in_=xs_raw[:].rearrange("p z (h l j) -> p (z h) j l", l=16, j=PACK),
-        )
+        def quantize(codes, plane, src, fmt):
+            nc.vector.quantize_mx(out=codes.bitcast(fmt), scales=plane, in_=src.rearrange("p c t -> p (c t)"))
+
+        quantize(warm_codes[:, N:], warm_plane[:, N:], warm_bf[:], E4M3)
+        for c0 in range(0, N, P):
+            quantize(warm_codes[:, c0 : c0 + P], warm_plane[:, c0 : c0 + P], warm_bf[:], E5M2)
+        for step in range(WARM_PASSES):
+            nc.tensor.matmul_mx(
+                out=w_ps[0][:],
+                lhsT=warm_codes[:, N:].bitcast(E4M3),
+                lhsT_scale=warm_plane[:, N:],
+                rhs=warm_codes[:, :N].bitcast(E5M2),
+                rhs_scale=warm_plane[:, :N],
+                start=True,
+                stop=True,
+            )
+
         nc.vector.tensor_copy(
             out=xt_dealt[:].rearrange("p j z (h l b) -> p (z h) j l b", l=8, b=2),
             in_=xt_raw[:].rearrange("p z (h l j b) -> p (z h) j l b", l=8, j=PACK, b=2),
+        )
+        nc.vector.tensor_copy(
+            out=xs_dealt[:].rearrange("p j z (h l) -> p (z h) j l", l=16),
+            in_=xs_raw[:].rearrange("p z (h l j) -> p (z h) j l", l=16, j=PACK),
         )
         nc.vector.tensor_copy(
             out=hs_dealt[:].rearrange("p i (h l b) -> p h i l b", l=8, b=2),
@@ -117,9 +145,6 @@ def tile_mix_wgrad_of_hidden_and_store_pl_kernel(
 
         def scalar_cast(out, in_):
             nc.scalar.activation(out=out, in_=in_, func=ACT.Copy)
-
-        def quantize(codes, plane, src, fmt):
-            nc.vector.quantize_mx(out=codes.bitcast(fmt), scales=plane, in_=src.rearrange("p c t -> p (c t)"))
 
         def first_layer(b):
             cols = slice(b * P, (b + 1) * P)
@@ -161,7 +186,7 @@ def tile_mix_wgrad_of_hidden_and_store_pl_kernel(
             first_layer(b)
             for i in range(PACK):
                 hidden(b, i)
-            if b == 0:
+            if b == 1:
                 nc.vector.tensor_copy(
                     out=hss_dealt[:].rearrange("p i (h l) -> p h i l", l=16),
                     in_=hss_raw[:, 0, :].rearrange("p (h l i) -> p h i l", l=16, i=PACK),
@@ -196,11 +221,18 @@ def tile_mix_wgrad_of_hidden_and_store_pl_kernel(
                 start=False,
                 stop=True,
             )
-            if i % 2 == 0:
-                nc.scalar.activation(out=y[:, i, :], in_=w_ps[i][:], func=ACT.Copy, scale=OUT_FACTOR)
-            else:
+            vector_cols = (0, N, 0, HALF)[i]
+            if vector_cols > 0:
                 nc.vector.tensor_scalar(
-                    out=y[:, i, :], in0=w_ps[i][:], scalar1=OUT_FACTOR, scalar2=None, op0=ALU.mult
+                    out=y[:, i, :vector_cols],
+                    in0=w_ps[i][:, :vector_cols],
+                    scalar1=OUT_FACTOR,
+                    scalar2=None,
+                    op0=ALU.mult,
+                )
+            if vector_cols < N:
+                nc.scalar.activation(
+                    out=y[:, i, vector_cols:], in_=w_ps[i][:, vector_cols:], func=ACT.Copy, scale=OUT_FACTOR
                 )
             nc.sync.dma_start(out=out_rows[:, i, :], in_=y[:, i, :])
 

@@ -22,8 +22,9 @@ PASSES = K // (P * PACK)
 QUADS = 4
 OUT_FACTOR = 0.04
 HALF = N // 2
-VECTOR_COLS = 384
-WARM_PASSES = 4
+VECTOR_COLS = 336
+WARM_PASSES = 3
+LATE_WARM_PASSES = 2
 
 
 def tile_mix_wgrad_of_hidden_and_store_pl_kernel(
@@ -124,14 +125,28 @@ def tile_mix_wgrad_of_hidden_and_store_pl_kernel(
                 stop=True,
             )
 
-        nc.vector.tensor_copy(
-            out=xt_dealt[:].rearrange("p j z (h l b) -> p (z h) j l b", l=8, b=2),
-            in_=xt_raw[:].rearrange("p z (h l j b) -> p (z h) j l b", l=8, j=PACK, b=2),
-        )
+        def deal_xt(slots):
+            nc.vector.tensor_copy(
+                out=xt_dealt[:].rearrange("p j z (h l b) -> p (z h) j l b", l=8, b=2)[:, :, slots],
+                in_=xt_raw[:].rearrange("p z (h l j b) -> p (z h) j l b", l=8, j=PACK, b=2)[:, :, slots],
+            )
+
+        deal_xt(slice(0, 2))
         nc.vector.tensor_copy(
             out=xs_dealt[:].rearrange("p j z (h l) -> p (z h) j l", l=16),
             in_=xs_raw[:].rearrange("p z (h l j) -> p (z h) j l", l=16, j=PACK),
         )
+        for step in range(LATE_WARM_PASSES):
+            nc.tensor.matmul_mx(
+                out=w_ps[0][:],
+                lhsT=warm_codes[:, N:].bitcast(E4M3),
+                lhsT_scale=warm_plane[:, N:],
+                rhs=xt_dealt[:, :2].rearrange("p j z c -> p (j z c)").bitcast(E2M1),
+                rhs_scale=xs_dealt[:, :2].rearrange("p j z c -> p (j z c)"),
+                start=True,
+                stop=True,
+            )
+        deal_xt(slice(2, 4))
         nc.vector.tensor_copy(
             out=hs_dealt[:].rearrange("p i (h l b) -> p h i l b", l=8, b=2),
             in_=hs_raw[:].rearrange("p (h l i b) -> p h i l b", l=8, i=PACK, b=2),
@@ -186,14 +201,15 @@ def tile_mix_wgrad_of_hidden_and_store_pl_kernel(
             first_layer(b)
             for i in range(PACK):
                 hidden(b, i)
-            if b == 1:
+            if b == 2:
                 nc.vector.tensor_copy(
                     out=hss_dealt[:].rearrange("p i (h l) -> p h i l", l=16),
                     in_=hss_raw[:, 0, :].rearrange("p (h l i) -> p h i l", l=16, i=PACK),
                 )
         quantize_g(0)
         first_layer(PACK - 1)
-        for i in range(PACK):
+
+        def stored_pass(i):
             nc.tensor.matmul_mx(
                 out=w_ps[i][:],
                 lhsT=hs_dealt[:, i, :].bitcast(E2M1),
@@ -203,15 +219,21 @@ def tile_mix_wgrad_of_hidden_and_store_pl_kernel(
                 start=True,
                 stop=False,
             )
+
         for i in range(PACK):
             hidden(PACK - 1, i)
             if i > 0:
                 quantize_ht(i - 1)
-        quantize_g(1)
+            if i == 1:
+                quantize_g(1)
         quantize_ht(PACK - 1)
 
         out_rows = out_0.rearrange("(p i) n -> p i n", i=PACK)
+        stored_pass(0)
+        stored_pass(1)
         for i in range(PACK):
+            if i + 2 < PACK:
+                stored_pass(i + 2)
             nc.tensor.matmul_mx(
                 out=w_ps[i][:],
                 lhsT=ht_codes[:, i, :].bitcast(E4M3),
@@ -221,19 +243,16 @@ def tile_mix_wgrad_of_hidden_and_store_pl_kernel(
                 start=False,
                 stop=True,
             )
-            vector_cols = (0, N, 0, HALF)[i]
-            if vector_cols > 0:
+            if i == 2:
                 nc.vector.tensor_scalar(
-                    out=y[:, i, :vector_cols],
-                    in0=w_ps[i][:, :vector_cols],
-                    scalar1=OUT_FACTOR,
-                    scalar2=None,
-                    op0=ALU.mult,
+                    out=y[:, i, :], in0=w_ps[i][:], scalar1=OUT_FACTOR, scalar2=None, op0=ALU.mult
                 )
-            if vector_cols < N:
-                nc.scalar.activation(
-                    out=y[:, i, vector_cols:], in_=w_ps[i][:, vector_cols:], func=ACT.Copy, scale=OUT_FACTOR
-                )
+            else:
+                step = HALF if i == PACK - 1 else N
+                for c0 in range(0, N, step):
+                    nc.scalar.activation(
+                        out=y[:, i, c0 : c0 + step], in_=w_ps[i][:, c0 : c0 + step], func=ACT.Copy, scale=OUT_FACTOR
+                    )
             nc.sync.dma_start(out=out_rows[:, i, :], in_=y[:, i, :])
 
         interleave(scalar_cast, y_bf[:, VECTOR_COLS:, :], y[:, :, VECTOR_COLS:])

@@ -22,7 +22,7 @@ PASSES = K // (P * PACK)
 QUADS = 4
 OUT_FACTOR = 0.04
 HALF = N // 2
-VECTOR_COLS = 336
+VECTOR_COLS = 320
 WARM_PASSES = 3
 LATE_WARM_PASSES = 2
 
@@ -87,15 +87,17 @@ def tile_mix_wgrad_of_hidden_and_store_pl_kernel(
             nc.vector.memset(plane[:].bitcast(U32), 0)
 
         nc.sync.dma_start(out=xt_raw[:].bitcast(I32), in_=xt_words.rearrange("z p c -> p z c").bitcast(I32))
-        for q in range(QUADS):
-            load_scale_rows(nc.scalar if q % 2 == 0 else nc.sync, xs_raw, xt_scales, q)
+        load_scale_rows(nc.scalar, xs_raw, xt_scales, 0)
+        load_scale_rows(nc.sync, xs_raw, xt_scales, 1)
+        load_scale_rows(nc.scalar, xs_raw, xt_scales, 2)
+        load_scale_rows(nc.sync, xs_raw, xt_scales, 3)
         load_scale_rows(nc.scalar, wa_plane, wa_scales, 0)
-        load_scale_rows(nc.sync, wa_plane, wa_scales, 1)
         nc.sync.dma_start(out=wa_codes[:].bitcast(I32), in_=wa_words.rearrange("z p c t -> p z (c t)").bitcast(I32))
+        nc.sync.dma_start(out=hs_raw[:].bitcast(I32), in_=hs_words[0].bitcast(I32))
+        load_scale_rows(nc.sync, wa_plane, wa_scales, 1)
         load_scale_rows(nc.sync, wa_plane, wa_scales, 2)
         load_scale_rows(nc.sync, wa_plane, wa_scales, 3)
         nc.sync.dma_start(out=rw_sb[:], in_=rw.rearrange("o (p j) -> p (o j)", j=PACK))
-        nc.sync.dma_start(out=hs_raw[:].bitcast(I32), in_=hs_words[0].bitcast(I32))
         load_g(0)
         load_scale_rows(nc.sync, hss_raw, hs_scales, 0)
         load_scale_rows(nc.sync, hss_raw, hs_scales, 1)
@@ -248,7 +250,7 @@ def tile_mix_wgrad_of_hidden_and_store_pl_kernel(
                     out=y[:, i, :], in0=w_ps[i][:], scalar1=OUT_FACTOR, scalar2=None, op0=ALU.mult
                 )
             else:
-                step = HALF if i == PACK - 1 else N
+                step = P if i == PACK - 1 else N
                 for c0 in range(0, N, step):
                     nc.scalar.activation(
                         out=y[:, i, c0 : c0 + step], in_=w_ps[i][:, c0 : c0 + step], func=ACT.Copy, scale=OUT_FACTOR
@@ -256,8 +258,9 @@ def tile_mix_wgrad_of_hidden_and_store_pl_kernel(
             nc.sync.dma_start(out=out_rows[:, i, :], in_=y[:, i, :])
 
         interleave(scalar_cast, y_bf[:, VECTOR_COLS:, :], y[:, :, VECTOR_COLS:])
-        interleave(nc.vector.tensor_copy, y_bf[:, :HALF, :], y[:, :, :HALF])
-        interleave(nc.vector.tensor_copy, y_bf[:, HALF:VECTOR_COLS, :], y[:, :, HALF:VECTOR_COLS])
+        for c0 in range(0, VECTOR_COLS, P):
+            cols = slice(c0, min(c0 + P, VECTOR_COLS))
+            interleave(nc.vector.tensor_copy, y_bf[:, cols, :], y[:, :, cols])
         word_rows = out_1[0].rearrange("p c t -> p (c t)").bitcast(I32)
         for h in range(2):
             cols = slice(h * HALF, (h + 1) * HALF)

from contextlib import ExitStack

import concourse.mybir as mybir

K, R, T, S, N = 1024, 512, 512, 512, 512
FLOPS = 2 * (K * R * T + T * R * N + S * R * N)

F32 = mybir.dt.float32
BF16 = mybir.dt.bfloat16
I32 = mybir.dt.int32
U32 = mybir.dt.uint32
U8 = mybir.dt.uint8
E4M3 = mybir.dt.float8_e4m3fn_x4
E5M2 = mybir.dt.float8_e5m2_x4
E2M1 = mybir.dt.float4_e2m1fn_x4
ALU = mybir.AluOpType
ACT = mybir.ActivationFunctionType

P = 128
PACK = 4
PASSES = K // (P * PACK)
QUADS = 4
OUT_FACTOR = 0.04
HALF = N // 2
VECTOR_COLS = 320
WARM_PASSES = 3
LATE_WARM_PASSES = 2


def tile_mix_wgrad_of_hidden_and_store_pl_kernel(
    tc, xt_words, xt_scales, wa_words, wa_scales, rw, g, hs_words, hs_scales, gs_words, gs_scales, out_0, out_1, out_2
):
    nc = tc.nc
    with ExitStack() as ctx:
        sb = ctx.enter_context(tc.tile_pool(name="sb", bufs=1))
        psum = ctx.enter_context(tc.psum_pool(name="psum", bufs=1))
        ctx.enter_context(tc.manual_schedule())

        def tile(name, shape, dtype):
            return sb.tile(shape, dtype, name=name, align_bytes=64)

        xt_raw = tile("xt_raw", [P, PASSES, 2 * T], U8)
        xt_dealt = tile("xt_dealt", [P, PACK, PASSES, 2 * P], U8)
        xs_raw = tile("xs_raw", [P, PASSES, T], U8)
        xs_dealt = tile("xs_dealt", [P, PACK, PASSES, P], U8)
        wa_codes = tile("wa_codes", [P, PASSES, R], U32)
        wa_plane = tile("wa_plane", [P, PASSES, R], U8)
        rw_sb = tile("rw_sb", [P, PACK], F32)
        g_raw = [tile("g_raw%d" % h, [P, PACK, HALF], F32) for h in range(2)]
        g_bf = tile("g_bf", [P, N, PACK], BF16)
        g_codes = tile("g_codes", [P, N], U32)
        g_plane = tile("g_plane", [P, N], U8)
        hs_raw = tile("hs_raw", [P, 2 * R], U8)
        hs_dealt = tile("hs_dealt", [P, PACK, 2 * P], U8)
        hss_raw = tile("hss_raw", [P, 1, R], U8)
        hss_dealt = tile("hss_dealt", [P, PACK, P], U8)
        gs_codes = tile("gs_codes", [P, N], U32)
        gs_plane = tile("gs_plane", [P, 1, N], U8)
        ht_bf = tile("ht_bf", [P, PACK, P, PACK], BF16)
        ht_codes = tile("ht_codes", [P, PACK, P], U32)
        ht_plane = tile("ht_plane", [P, PACK, P], U8)
        y = tile("y", [P, PACK, N], F32)
        y_bf = tile("y_bf", [P, N, PACK], BF16)
        y_codes = tile("y_codes", [P, N], U32)
        y_plane = tile("y_plane", [P, N], U8)
        warm_bf = tile("warm_bf", [P, P, PACK], BF16)
        warm_codes = tile("warm_codes", [P, N + P], U32)
        warm_plane = tile("warm_plane", [P, N + P], U8)
        a_ps = [psum.tile([P, PACK, P], F32, name="a_ps%d" % b) for b in range(PACK)]
        w_ps = [psum.tile([P, N], F32, name="w_ps%d" % i) for i in range(PACK)]

        def load_scale_rows(queue, plane, scales, q):
            queue.dma_start(
                out=plane[32 * q : 32 * q + 4].bitcast(I32),
                in_=scales[:, 4 * q : 4 * q + 4, :].rearrange("z r c -> r z c").bitcast(I32),
            )

        def load_g(h):
            nc.sync.dma_start(
                out=g_raw[h][:], in_=g.rearrange("(p j) n -> p j n", j=PACK)[:, :, h * HALF : (h + 1) * HALF]
            )

        for plane in (xs_raw, wa_plane):
            nc.vector.memset(plane[:].bitcast(U32), 0)
        nc.vector.memset(warm_bf[:].rearrange("p c t -> p (c t)").bitcast(U32), 0)
        for plane in (hss_raw, gs_plane):
            nc.vector.memset(plane[:].bitcast(U32), 0)

        nc.sync.dma_start(out=xt_raw[:].bitcast(I32), in_=xt_words.rearrange("z p c -> p z c").bitcast(I32))
        load_scale_rows(nc.scalar, xs_raw, xt_scales, 0)
        load_scale_rows(nc.sync, xs_raw, xt_scales, 1)
        load_scale_rows(nc.scalar, xs_raw, xt_scales, 2)
        load_scale_rows(nc.sync, xs_raw, xt_scales, 3)
        load_scale_rows(nc.scalar, wa_plane, wa_scales, 0)
        nc.sync.dma_start(out=wa_codes[:].bitcast(I32), in_=wa_words.rearrange("z p c t -> p z (c t)").bitcast(I32))
        nc.sync.dma_start(out=hs_raw[:].bitcast(I32), in_=hs_words[0].bitcast(I32))
        load_scale_rows(nc.sync, wa_plane, wa_scales, 1)
        load_scale_rows(nc.sync, wa_plane, wa_scales, 2)
        load_scale_rows(nc.sync, wa_plane, wa_scales, 3)
        nc.sync.dma_start(out=rw_sb[:], in_=rw.rearrange("o (p j) -> p (o j)", j=PACK))
        load_g(0)
        load_scale_rows(nc.sync, hss_raw, hs_scales, 0)
        load_scale_rows(nc.sync, hss_raw, hs_scales, 1)
        load_g(1)
        load_scale_rows(nc.sync, hss_raw, hs_scales, 2)
        load_scale_rows(nc.sync, hss_raw, hs_scales, 3)
        load_scale_rows(nc.sync, gs_plane, gs_scales, 0)
        load_scale_rows(nc.sync, gs_plane, gs_scales, 1)
        nc.sync.dma_start(out=gs_codes[:].bitcast(I32), in_=gs_words[0].rearrange("p c t -> p (c t)").bitcast(I32))
        load_scale_rows(nc.sync, gs_plane, gs_scales, 2)
        load_scale_rows(nc.sync, gs_plane, gs_scales, 3)

        def quantize(codes, plane, src, fmt):
            nc.vector.quantize_mx(out=codes.bitcast(fmt), scales=plane, in_=src.rearrange("p c t -> p (c t)"))

        quantize(warm_codes[:, N:], warm_plane[:, N:], warm_bf[:], E4M3)
        for c0 in range(0, N, P):
            quantize(warm_codes[:, c0 : c0 + P], warm_plane[:, c0 : c0 + P], warm_bf[:], E5M2)
        for step in range(WARM_PASSES):
            nc.tensor.matmul_mx(
                out=w_ps[0][:],
                lhsT=warm_codes[:, N:].bitcast(E4M3),
                lhsT_scale=warm_plane[:, N:],
                rhs=warm_codes[:, :N].bitcast(E5M2),
                rhs_scale=warm_plane[:, :N],
                start=True,
                stop=True,
            )

        def deal_xt(slots):
            nc.vector.tensor_copy(
                out=xt_dealt[:].rearrange("p j z (h l b) -> p (z h) j l b", l=8, b=2)[:, :, slots],
                in_=xt_raw[:].rearrange("p z (h l j b) -> p (z h) j l b", l=8, j=PACK, b=2)[:, :, slots],
            )

        deal_xt(slice(0, 2))
        nc.vector.tensor_copy(
            out=xs_dealt[:].rearrange("p j z (h l) -> p (z h) j l", l=16),
            in_=xs_raw[:].rearrange("p z (h l j) -> p (z h) j l", l=16, j=PACK),
        )
        for step in range(LATE_WARM_PASSES):
            nc.tensor.matmul_mx(
                out=w_ps[0][:],
                lhsT=warm_codes[:, N:].bitcast(E4M3),
                lhsT_scale=warm_plane[:, N:],
                rhs=xt_dealt[:, :2].rearrange("p j z c -> p (j z c)").bitcast(E2M1),
                rhs_scale=xs_dealt[:, :2].rearrange("p j z c -> p (j z c)"),
                start=True,
                stop=True,
            )
        deal_xt(slice(2, 4))
        nc.vector.tensor_copy(
            out=hs_dealt[:].rearrange("p i (h l b) -> p h i l b", l=8, b=2),
            in_=hs_raw[:].rearrange("p (h l i b) -> p h i l b", l=8, i=PACK, b=2),
        )

        def interleave(copy, dst, src):
            copy(
                out=dst.rearrange("p (c e) t -> p c t e", e=4),
                in_=src.rearrange("p t (c e) -> p c t e", e=4),
            )

        def scalar_cast(out, in_):
            nc.scalar.activation(out=out, in_=in_, func=ACT.Copy)

        def first_layer(b):
            cols = slice(b * P, (b + 1) * P)
            for j in range(PACK):
                for z in range(PASSES):
                    nc.tensor.matmul_mx(
                        out=a_ps[b][:, j, :],
                        lhsT=xt_dealt[:, j, z, :].bitcast(E2M1),
                        lhsT_scale=xs_dealt[:, j, z, :],
                        rhs=wa_codes[:, z, cols].bitcast(E4M3),
                        rhs_scale=wa_plane[:, z, cols],
                        start=(z == 0),
                        stop=(z == PASSES - 1),
                    )

        per_bank = P // PACK

        def hidden(b, i):
            nc.vector.scalar_tensor_tensor(
                out=ht_bf[:, i, b * per_bank : (b + 1) * per_bank, :],
                in0=a_ps[b][:].rearrange("p j (m i) -> p i m j", i=PACK)[:, i],
                scalar=0.0,
                in1=rw_sb[:].unsqueeze(1).to_broadcast([P, per_bank, PACK]),
                op0=ALU.max,
                op1=ALU.mult,
            )

        def quantize_g(h):
            cols = slice(h * HALF, (h + 1) * HALF)
            quantize(g_codes[:, cols], g_plane[:, cols], g_bf[:, cols, :], E5M2)

        def quantize_ht(i):
            quantize(ht_codes[:, i, :], ht_plane[:, i, :], ht_bf[:, i], E4M3)

        for h in range(2):
            interleave(scalar_cast, g_bf[:, h * HALF : (h + 1) * HALF, :], g_raw[h][:])

        for b in range(PACK - 1):
            first_layer(b)
            for i in range(PACK):
                hidden(b, i)
            if b == 2:
                nc.vector.tensor_copy(
                    out=hss_dealt[:].rearrange("p i (h l) -> p h i l", l=16),
                    in_=hss_raw[:, 0, :].rearrange("p (h l i) -> p h i l", l=16, i=PACK),
                )
        quantize_g(0)
        first_layer(PACK - 1)

        def stored_pass(i):
            nc.tensor.matmul_mx(
                out=w_ps[i][:],
                lhsT=hs_dealt[:, i, :].bitcast(E2M1),
                lhsT_scale=hss_dealt[:, i, :],
                rhs=gs_codes[:].bitcast(E4M3),
                rhs_scale=gs_plane[:, 0, :],
                start=True,
                stop=False,
            )

        for i in range(PACK):
            hidden(PACK - 1, i)
            if i > 0:
                quantize_ht(i - 1)
            if i == 1:
                quantize_g(1)
        quantize_ht(PACK - 1)

        out_rows = out_0.rearrange("(p i) n -> p i n", i=PACK)
        stored_pass(0)
        stored_pass(1)
        for i in range(PACK):
            if i + 2 < PACK:
                stored_pass(i + 2)
            nc.tensor.matmul_mx(
                out=w_ps[i][:],
                lhsT=ht_codes[:, i, :].bitcast(E4M3),
                lhsT_scale=ht_plane[:, i, :],
                rhs=g_codes[:].bitcast(E5M2),
                rhs_scale=g_plane[:],
                start=False,
                stop=True,
            )
            if i == 2:
                nc.vector.tensor_scalar(
                    out=y[:, i, :], in0=w_ps[i][:], scalar1=OUT_FACTOR, scalar2=None, op0=ALU.mult
                )
            else:
                step = P if i == PACK - 1 else N
                for c0 in range(0, N, step):
                    nc.scalar.activation(
                        out=y[:, i, c0 : c0 + step], in_=w_ps[i][:, c0 : c0 + step], func=ACT.Copy, scale=OUT_FACTOR
                    )
            nc.sync.dma_start(out=out_rows[:, i, :], in_=y[:, i, :])

        interleave(scalar_cast, y_bf[:, VECTOR_COLS:, :], y[:, :, VECTOR_COLS:])
        for c0 in range(0, VECTOR_COLS, P):
            cols = slice(c0, min(c0 + P, VECTOR_COLS))
            interleave(nc.vector.tensor_copy, y_bf[:, cols, :], y[:, :, cols])
        word_rows = out_1[0].rearrange("p c t -> p (c t)").bitcast(I32)
        for h in range(2):
            cols = slice(h * HALF, (h + 1) * HALF)
            quantize(y_codes[:, cols], y_plane[:, cols], y_bf[:, cols, :], E4M3)
            nc.sync.dma_start(out=word_rows[:, cols], in_=y_codes[:, cols].bitcast(I32))
        for q in range(QUADS):
            queue = nc.scalar if q % 2 == 0 else nc.sync
            queue.dma_start(
                out=out_2[0, 4 * q : 4 * q + 4, :].bitcast(I32), in_=y_plane[32 * q : 32 * q + 4, :].bitcast(I32)
            )
